import numpy as np
import ml_dtypes


def mxq(x, axis, fmt="e4m3"):
    dtype, down = {"e4m3": (ml_dtypes.float8_e4m3fn, 7), "e5m2": (ml_dtypes.float8_e5m2, 14)}[fmt]
    v = np.moveaxis(np.asarray(x, np.float32).astype(ml_dtypes.bfloat16).astype(np.float64), axis, -1)
    blocks = v.reshape(v.shape[:-1] + (-1, 32))
    amax = np.abs(blocks).max(-1, keepdims=True)
    byte = np.maximum(np.where(amax > 0, np.frexp(amax)[1] - 1 + 127, 0) - down, 1)
    scale = np.exp2(byte - 127.0)
    codes = (blocks / scale).astype(np.float32).astype(dtype).astype(np.float64)
    return np.moveaxis((codes * scale).reshape(v.shape), -1, axis)


WIDE = False


def mx_kscale(k):
    if not WIDE:
        return np.ones(k)
    levels = np.array([10, -10, 5, -5, 0])
    if k % 512:
        return np.exp2(np.random.permutation(np.resize(levels, k // 32))).repeat(32)
    a = np.empty((k // 512, 16))
    for p in range(k // 512):
        a[p, :8] = np.random.permutation(np.resize(levels, 8))
        for g in range(8):
            far = levels[np.abs(levels - a[p, g]) >= 10]
            a[p, g + 8] = far[np.random.randint(len(far))]
    return np.exp2(a.ravel()).repeat(32)


def f64(x):
    return np.asarray(x).astype(np.float64)


def striped(idx):
    return np.tile(idx.reshape(-1, 16).T, (8, 1)).astype(np.uint16)


def unstriped(offs):
    return offs[:16].T.reshape(-1).astype(np.int64)


def striped8(idx):
    return np.concatenate([x.reshape(-1, 16).T for x in idx]).astype(np.uint16)


def runs(offs, k):
    lists = np.stack([offs[16 * r : 16 * r + 16].T.reshape(-1) for r in range(8)]).astype(np.int64)
    return lists[np.arange(k) % 512 // 64]


def pack_weight(w):
    k, n = w.shape
    w = f64(np.asarray(w, np.float32).astype(ml_dtypes.bfloat16)).reshape(k // 32, 32, n)
    amax = np.abs(w).max(1)
    byte = np.clip(np.where(amax > 0, np.frexp(amax)[1] - 1 + 127 - 7, 1), 1, 254)
    scaled = (w * np.exp2(127.0 - byte)[:, None, :]).reshape(k, n).astype(np.float32)
    words = np.ascontiguousarray(scaled.reshape(k // 512, 128, 4, n).transpose(0, 1, 3, 2)).astype(ml_dtypes.float8_e4m3fn).view(np.uint8)
    return words, np.ascontiguousarray(byte.astype(np.uint8).reshape(k // 512, 16, n))


def unpack_weight(words, scales):
    g, p, n, _ = words.shape
    vals = np.ascontiguousarray(words).view(ml_dtypes.float8_e4m3fn).astype(np.float64) * np.repeat(np.exp2(scales.astype(np.float64) - 127.0), 8, axis=1)[..., None]
    return vals.transpose(0, 1, 3, 2).reshape(g * 512, n)


K, T, S, N, U, H = 512, 2048, 512, 512, 1024, 512


def setup_inputs():
    n = np.random.standard_normal
    s = mx_kscale(K)[:, None]
    u = mx_kscale(H)
    packed_xT = pack_weight(n((K, T)) * s)
    return {
        "x_words": packed_xT[0],
        "x_scales": packed_xT[1],
        "w1": (n((K, H)) / np.sqrt(K) / s * u).astype(np.float32),
        "w2": (n((K, H)) / np.sqrt(K) / s).astype(np.float32),
        "one": np.random.uniform(0.5, 1.5, (H, U)).astype(np.float32),
        "w3": (n((H, N)) / np.sqrt(H) / u[:, None]).astype(np.float32),
        "offs": striped(np.random.permutation(T)[:S]),
        "h1": striped8(np.stack([np.random.permutation(U)[:S] for _ in range(8)])),
        "h2": striped8(np.stack([np.random.permutation(U)[:S] for _ in range(8)])),
    }


def reference(x_words, x_scales, w1, w2, one, w3, offs, h1, h2):
    xq = unpack_weight(x_words, x_scales)[:, unstriped(offs)]
    y = mxq(f64(w1), 0, "e4m3").T @ xq
    s1 = np.zeros((H, U))
    s1[np.arange(H)[:, None], runs(h1, H)] = y
    e = mxq(f64(w2), 0, "e4m3").T @ xq
    s2 = f64(one).copy()
    s2[np.arange(H)[:, None], runs(h2, H)] = e
    z = s1 * s2
    return mxq(f64(w3), 0, "e4m3").T @ mxq(z, 0, "e4m3")

@@ -1,0 +1,188 @@
+from contextlib import ExitStack
+
+import concourse.mybir as mybir
+
+K, T, S, N, U, H = 512, 2048, 512, 512, 1024, 512
+FLOPS = 2 * (2 * K * H * S + H * N * U)
+
+F32 = mybir.dt.float32
+BF16 = mybir.dt.bfloat16
+I32 = mybir.dt.int32
+U32 = mybir.dt.uint32
+U16 = mybir.dt.uint16
+U8 = mybir.dt.uint8
+FP8X4 = mybir.dt.float8_e4m3fn_x4
+MULT = mybir.AluOpType.mult
+
+P = 128
+PACK = 4
+HALF = S // 2
+BANK = 512
+CHUNKS = (128, 128, 256, 256, 128, 128)
+
+
+def tile_picked_tsketch_none_p_kernel(
+    tc, x_words, x_scales, w1, w2, one, w3, offs, h1, h2, out
+):
+    nc = tc.nc
+    with ExitStack() as ctx:
+        keep = ctx.enter_context(tc.tile_pool(name="keep", bufs=1))
+        psum = ctx.enter_context(tc.psum_pool(name="psum", bufs=8))
+
+        def sb(name, shape, dtype, tag=None):
+            return keep.tile(shape, dtype, name=name, tag=tag or name, align_bytes=64)
+
+        def plane_rows(a, t):
+            return a.rearrange("(g t r) c -> t g r c", t=PACK, r=8)[t]
+
+        offs_sb = keep.tile([P, S // 16], U16, name="offs_sb")
+        h1_sb = keep.tile([P, S // 16], U16, name="h1_sb")
+        h2_sb = keep.tile([P, S // 16], U16, name="h2_sb")
+        xs_all = sb("xs_all", [P, T], U8)
+        xw_all = sb("xw_all", [P, T], U32)
+        w1_raw = sb("w1_raw", [P, PACK, H], F32)
+        w2_raw = sb("w2_raw", [P, PACK, H], F32, tag="w2_then_y3")
+        w3_raw = sb("w3_raw", [P, PACK, N], F32, tag="w3_then_e2")
+        s1 = [sb("s1_%d" % t, [P, 2 * U if t == 2 else U], F32) for t in range(PACK)]
+        s2 = [sb("s2_%d" % t, [P, 2 * U if t == 2 else U], F32) for t in range(PACK)]
+
+        nc.vector.memset(xs_all[:].bitcast(I32), 0)
+        nc.sync.dma_start(offs_sb[:], offs)
+        nc.sync.dma_start(w1_raw[:], w1.rearrange("(p j) c -> p j c", j=PACK))
+        for q in range(4):
+            nc.sync.dma_start(
+                xs_all[32 * q : 32 * q + 4, :].bitcast(I32), x_scales[0, 4 * q : 4 * q + 4, :].bitcast(I32)
+            )
+        nc.sync.dma_start(xw_all[:].bitcast(I32), x_words[0].rearrange("p n t -> p (n t)").bitcast(I32))
+        nc.sync.dma_start(h1_sb[:], h1)
+        nc.sync.dma_start(w2_raw[:], w2.rearrange("(p j) c -> p j c", j=PACK))
+        nc.sync.dma_start(h2_sb[:], h2)
+        for t in (0, 1):
+            nc.sync.dma_start(s2[t][:, 0:U], plane_rows(one, t))
+        for t in range(PACK):
+            nc.sync.dma_start(w3_raw[:, t, :], plane_rows(w3, t))
+        for t in (3, 2):
+            nc.sync.dma_start(s2[t][:, 0:U], plane_rows(one, t))
+        for t in (0, 1, 3, 2):
+            nc.gpsimd.memset(s1[t][:, 0:U], 0.0)
+
+        def planes(name, width):
+            return sb(name + "_codes", [P, width], U32), sb(name + "_scales", [P, width], U8)
+
+        def quantize_into(q, lo, hi, grouped):
+            nc.vector.quantize_mx(out=q[0][:, lo:hi].bitcast(FP8X4), scales=q[1][:, lo:hi], in_=grouped)
+
+        def quantize(name, grouped, width):
+            q = planes(name, width)
+            quantize_into(q, 0, width, grouped)
+            return q
+
+        def deal(copy, grouped, raw, t0, t1):
+            copy(
+                grouped[:].rearrange("p (t g r j) -> p t g r j", t=PACK, r=8, j=PACK)[:, t0:t1],
+                raw[:].rearrange("p j (g t r) -> p t g r j", t=PACK, r=8)[:, t0:t1],
+            )
+
+        def product(weights, cols, moving, mcols, acc):
+            nc.tensor.matmul_mx(
+                out=acc,
+                lhsT=weights[0][:, cols].bitcast(FP8X4),
+                lhsT_scale=weights[1][:, cols],
+                rhs=moving[0][:, mcols].bitcast(FP8X4),
+                rhs_scale=moving[1][:, mcols],
+                start=True,
+                stop=True,
+            )
+
+        xs = sb("xs", [P, S], U8)
+        xw = sb("xw", [P, S], U32)
+        nc.vector.tensor_copy(xs[:], xs_all[:].indirect(offs_sb[:]))
+        w1_bf = sb("w1_bf", [P, PACK * H], BF16)
+        deal(nc.vector.tensor_copy, w1_bf, w1_raw, 0, 2)
+        w1q = planes("w1", H)
+        quantize_into(w1q, 0, H // 2, w1_bf[:, 0 : 2 * H])
+        deal(nc.scalar.copy, w1_bf, w1_raw, 2, 4)
+        quantize_into(w1q, H // 2, H, w1_bf[:, 2 * H : 4 * H])
+        for h in range(2):
+            nc.vector.tensor_copy(
+                xw[:, h * HALF : (h + 1) * HALF], xw_all[:].indirect(offs_sb[:, h * 16 : (h + 1) * 16])
+            )
+        xq = (xw, xs)
+
+        def project(name, weights, t, lo, hi, tag=None):
+            acc = psum.tile([P, BANK], F32, name="acc", tag="acc")
+            product(weights, slice(t * P, (t + 1) * P), xq, slice(lo, hi), acc[:, 0 : hi - lo])
+            vals = sb(name, [P, hi - lo], F32, tag=tag)
+            nc.scalar.copy(vals[:], acc[:, 0 : hi - lo])
+            return vals
+
+        def scatter(window, lists, vals, lo, hi):
+            nc.vector.tensor_copy(window[:].indirect(lists[:, lo // 16 : hi // 16]), vals[:])
+
+        for h in range(2):
+            for t in range(2):
+                lo, hi = h * HALF, (h + 1) * HALF
+                scatter(s1[t], h1_sb, project("y%d_%d" % (t, h), w1q, t, lo, hi), lo, hi)
+
+        w2_bf = sb("w2_bf", [P, PACK * H], BF16)
+        deal(nc.scalar.copy, w2_bf, w2_raw, 0, 2)
+        deal(nc.scalar.copy, w2_bf, w2_raw, 2, 4)
+        w2q = quantize("w2", w2_bf[:], H)
+        scatter(s1[3], h1_sb, project("y3", w1q, 3, 0, S, tag="w2_then_y3"), 0, S)
+
+        early = CHUNKS[0] + CHUNKS[1]
+        z01 = [sb("z01_a", [P, 2, early], BF16, tag="z01_then_y2"), sb("z01_b", [P, 2, U - early], BF16)]
+        for t in range(2):
+            scatter(s2[t], h2_sb, project("e%d" % t, w2q, t, 0, S), 0, S)
+            nc.gpsimd.tensor_tensor(z01[0][:, t, :], s1[t][:, 0:early], s2[t][:, 0:early], MULT)
+            nc.gpsimd.tensor_tensor(z01[1][:, t, :], s1[t][:, early:U], s2[t][:, early:U], MULT)
+        scatter(s2[3], h2_sb, project("e3", w2q, 3, 0, S), 0, S)
+        w3_bf = sb("w3_bf", [P, PACK * N], BF16)
+        nc.scalar.copy(
+            w3_bf[:].rearrange("p (m t) -> p m t", t=PACK), w3_raw[:].rearrange("p t m -> p m t")
+        )
+        w3q = quantize("w3", w3_bf[:], N)
+
+        e2 = project("e2", w2q, 2, 0, S, tag="w3_then_e2")
+        nc.scalar.copy(s2[2][:, U : 2 * U], s1[3][:])
+        scatter(s2[2], h2_sb, e2, 0, S)
+        nc.scalar.copy(s1[2][:, U : 2 * U], s2[3][:])
+
+        starts = [sum(CHUNKS[:c]) for c in range(len(CHUNKS))]
+        z = [sb("z_%d" % c, [P, width, PACK], BF16) for c, width in enumerate(CHUNKS)]
+        for c, width in enumerate(CHUNKS):
+            part, first = (z01[0], starts[c]) if c < 2 else (z01[1], starts[c] - early)
+            nc.scalar.copy(z[c][:, :, 0:2], part[:, :, first : first + width].rearrange("p u w -> p w u"))
+            if c == 1:
+                scatter(s1[2], h1_sb, project("y2", w1q, 2, 0, S, tag="z01_then_y2"), 0, S)
+
+        pair1 = s1[2][:].rearrange("p (u w) -> p w u", u=2)
+        pair2 = s2[2][:].rearrange("p (u w) -> p w u", u=2)
+        out_rows = out.rearrange("(mt p) w -> p mt w", p=P)
+
+        def multiply(c):
+            cols = slice(starts[c], starts[c] + CHUNKS[c])
+            nc.vector.tensor_tensor(z[c][:, :, 2:4], pair1[:, cols, :], pair2[:, cols, :], MULT)
+
+        def layer(c):
+            width = CHUNKS[c]
+            cols = slice(starts[c], starts[c] + width)
+            zq = quantize("z%d" % c, z[c][:].rearrange("p w t -> p (w t)"), width)
+            per_bank = BANK // width
+            for m0 in range(0, N // P, per_bank):
+                acc = psum.tile([P, BANK], F32, name="acc", tag="acc")
+                for i in range(per_bank):
+                    mt = m0 + i
+                    product(w3q, slice(mt * P, (mt + 1) * P), zq, slice(0, width), acc[:, i * width : (i + 1) * width])
+                res = sb("res_%d_%d" % (c, m0), [P, BANK], F32)
+                copy = nc.vector.tensor_copy if c >= len(CHUNKS) - 2 else nc.scalar.copy
+                copy(res[:], acc[:])
+                nc.sync.dma_start(
+                    out_rows[:, m0 : m0 + per_bank, cols], res[:].rearrange("p (i w) -> p i w", w=width)
+                )
+
+        multiply(0)
+        for c in range(1, len(CHUNKS)):
+            multiply(c)
+            layer(c - 1)
+        layer(len(CHUNKS) - 1)

@@ -18,7 +18,7 @@ P = 128
 PACK = 4
 HALF = S // 2
 BANK = 512
-CHUNKS = (128, 128, 256, 256, 128, 128)
+CHUNKS = (256, 256, 256, 128, 128)
 
 
 def tile_picked_tsketch_none_p_kernel(
@@ -41,10 +41,10 @@ def tile_picked_tsketch_none_p_kernel(
         xs_all = sb("xs_all", [P, T], U8)
         xw_all = sb("xw_all", [P, T], U32)
         w1_raw = sb("w1_raw", [P, PACK, H], F32)
-        w2_raw = sb("w2_raw", [P, PACK, H], F32, tag="w2_then_y3")
-        w3_raw = sb("w3_raw", [P, PACK, N], F32, tag="w3_then_e2")
-        s1 = [sb("s1_%d" % t, [P, 2 * U if t == 2 else U], F32) for t in range(PACK)]
-        s2 = [sb("s2_%d" % t, [P, 2 * U if t == 2 else U], F32) for t in range(PACK)]
+        w2_raw = sb("w2_raw", [P, PACK, H], F32, tag="w2_then_s2")
+        w3_raw = sb("w3_raw", [P, PACK, N], F32)
+        s1 = [sb("s1_%d" % t, [P, PACK * U if t == 0 else U], F32) for t in range(PACK)]
+        s2 = [None] + [sb("s2_%d" % t, [P, U], F32) for t in range(1, PACK)]
 
         nc.vector.memset(xs_all[:].bitcast(I32), 0)
         nc.sync.dma_start(offs_sb[:], offs)
@@ -57,14 +57,13 @@ def tile_picked_tsketch_none_p_kernel(
         nc.sync.dma_start(h1_sb[:], h1)
         nc.sync.dma_start(w2_raw[:], w2.rearrange("(p j) c -> p j c", j=PACK))
         nc.sync.dma_start(h2_sb[:], h2)
-        for t in (0, 1):
-            nc.sync.dma_start(s2[t][:, 0:U], plane_rows(one, t))
+        nc.sync.dma_start(s2[3][:], plane_rows(one, 3))
         for t in range(PACK):
             nc.sync.dma_start(w3_raw[:, t, :], plane_rows(w3, t))
-        for t in (3, 2):
-            nc.sync.dma_start(s2[t][:, 0:U], plane_rows(one, t))
-        for t in (0, 1, 3, 2):
-            nc.gpsimd.memset(s1[t][:, 0:U], 0.0)
+        for t in (2, 1):
+            nc.sync.dma_start(s2[t][:], plane_rows(one, t))
+        for t in (2, 3, 1, 0):
+            nc.vector.memset(s1[t][:, 0:U], 0.0)
 
         def planes(name, width):
             return sb(name + "_codes", [P, width], U32), sb(name + "_scales", [P, width], U8)
@@ -98,29 +97,31 @@ def tile_picked_tsketch_none_p_kernel(
         xw = sb("xw", [P, S], U32)
         nc.vector.tensor_copy(xs[:], xs_all[:].indirect(offs_sb[:]))
         w1_bf = sb("w1_bf", [P, PACK * H], BF16)
-        deal(nc.vector.tensor_copy, w1_bf, w1_raw, 0, 2)
         w1q = planes("w1", H)
-        quantize_into(w1q, 0, H // 2, w1_bf[:, 0 : 2 * H])
-        deal(nc.scalar.copy, w1_bf, w1_raw, 2, 4)
+        deal(nc.vector.tensor_copy, w1_bf, w1_raw, 2, 4)
         quantize_into(w1q, H // 2, H, w1_bf[:, 2 * H : 4 * H])
+        deal(nc.scalar.copy, w1_bf, w1_raw, 0, 2)
+        quantize_into(w1q, 0, H // 2, w1_bf[:, 0 : 2 * H])
         for h in range(2):
             nc.vector.tensor_copy(
                 xw[:, h * HALF : (h + 1) * HALF], xw_all[:].indirect(offs_sb[:, h * 16 : (h + 1) * 16])
             )
         xq = (xw, xs)
 
-        def project(name, weights, t, lo, hi, tag=None):
+        def project(name, weights, t, lo, hi, vals=None):
             acc = psum.tile([P, BANK], F32, name="acc", tag="acc")
             product(weights, slice(t * P, (t + 1) * P), xq, slice(lo, hi), acc[:, 0 : hi - lo])
-            vals = sb(name, [P, hi - lo], F32, tag=tag)
-            nc.scalar.copy(vals[:], acc[:, 0 : hi - lo])
+            if vals is None:
+                tile = sb(name, [P, hi - lo], F32)
+                vals = tile[:]
+            nc.scalar.copy(vals, acc[:, 0 : hi - lo])
             return vals
 
         def scatter(window, lists, vals, lo, hi):
-            nc.vector.tensor_copy(window[:].indirect(lists[:, lo // 16 : hi // 16]), vals[:])
+            nc.vector.tensor_copy(window[:].indirect(lists[:, lo // 16 : hi // 16]), vals)
 
         for h in range(2):
-            for t in range(2):
+            for t in (2, 3):
                 lo, hi = h * HALF, (h + 1) * HALF
                 scatter(s1[t], h1_sb, project("y%d_%d" % (t, h), w1q, t, lo, hi), lo, hi)
 
@@ -128,55 +129,52 @@ def tile_picked_tsketch_none_p_kernel(
         deal(nc.scalar.copy, w2_bf, w2_raw, 0, 2)
         deal(nc.scalar.copy, w2_bf, w2_raw, 2, 4)
         w2q = quantize("w2", w2_bf[:], H)
-        scatter(s1[3], h1_sb, project("y3", w1q, 3, 0, S, tag="w2_then_y3"), 0, S)
+        s2[0] = sb("s2_0", [P, PACK * U], F32, tag="w2_then_s2")
+        nc.sync.dma_start(s2[0][:, 0:U], plane_rows(one, 0))
+        scatter(s1[1], h1_sb, project("y1", w1q, 1, 0, S, vals=s2[0][:, U : U + S]), 0, S)
 
-        early = CHUNKS[0] + CHUNKS[1]
-        z01 = [sb("z01_a", [P, 2, early], BF16, tag="z01_then_y2"), sb("z01_b", [P, 2, U - early], BF16)]
-        for t in range(2):
-            scatter(s2[t], h2_sb, project("e%d" % t, w2q, t, 0, S), 0, S)
-            nc.gpsimd.tensor_tensor(z01[0][:, t, :], s1[t][:, 0:early], s2[t][:, 0:early], MULT)
-            nc.gpsimd.tensor_tensor(z01[1][:, t, :], s1[t][:, early:U], s2[t][:, early:U], MULT)
-        scatter(s2[3], h2_sb, project("e3", w2q, 3, 0, S), 0, S)
         w3_bf = sb("w3_bf", [P, PACK * N], BF16)
         nc.scalar.copy(
             w3_bf[:].rearrange("p (m t) -> p m t", t=PACK), w3_raw[:].rearrange("p t m -> p m t")
         )
         w3q = quantize("w3", w3_bf[:], N)
 
-        e2 = project("e2", w2q, 2, 0, S, tag="w3_then_e2")
-        nc.scalar.copy(s2[2][:, U : 2 * U], s1[3][:])
-        scatter(s2[2], h2_sb, e2, 0, S)
-        nc.scalar.copy(s1[2][:, U : 2 * U], s2[3][:])
+        for t in (3, 2, 1):
+            scatter(s2[t], h2_sb, project("e%d" % t, w2q, t, 0, S), 0, S)
+        e0 = project("e0", w2q, 0, 0, S)
+        y0 = project("y0", w1q, 0, 0, S)
+        for t in (2, 3, 1):
+            nc.scalar.copy(s2[0][:, t * U : (t + 1) * U], s1[t][:])
+        scatter(s2[0], h2_sb, e0, 0, S)
+        for t in (3, 2, 1):
+            nc.scalar.copy(s1[0][:, t * U : (t + 1) * U], s2[t][:])
+        scatter(s1[0], h1_sb, y0, 0, S)
 
         starts = [sum(CHUNKS[:c]) for c in range(len(CHUNKS))]
-        z = [sb("z_%d" % c, [P, width, PACK], BF16) for c, width in enumerate(CHUNKS)]
-        for c, width in enumerate(CHUNKS):
-            part, first = (z01[0], starts[c]) if c < 2 else (z01[1], starts[c] - early)
-            nc.scalar.copy(z[c][:, :, 0:2], part[:, :, first : first + width].rearrange("p u w -> p w u"))
-            if c == 1:
-                scatter(s1[2], h1_sb, project("y2", w1q, 2, 0, S, tag="z01_then_y2"), 0, S)
-
-        pair1 = s1[2][:].rearrange("p (u w) -> p w u", u=2)
-        pair2 = s2[2][:].rearrange("p (u w) -> p w u", u=2)
+        z = [sb("z_%d" % c, [P, width * PACK], BF16) for c, width in enumerate(CHUNKS)]
+        left = s1[0][:].rearrange("p (t a i) -> p a t i", t=PACK, i=4)
+        right = s2[0][:].rearrange("p (t a i) -> p a t i", t=PACK, i=4)
         out_rows = out.rearrange("(mt p) w -> p mt w", p=P)
 
         def multiply(c):
-            cols = slice(starts[c], starts[c] + CHUNKS[c])
-            nc.vector.tensor_tensor(z[c][:, :, 2:4], pair1[:, cols, :], pair2[:, cols, :], MULT)
+            quads = slice(starts[c] // 4, (starts[c] + CHUNKS[c]) // 4)
+            nc.vector.tensor_tensor(
+                z[c][:].rearrange("p (a i t) -> p a t i", t=PACK, i=4), left[:, quads], right[:, quads], MULT
+            )
 
         def layer(c):
             width = CHUNKS[c]
             cols = slice(starts[c], starts[c] + width)
-            zq = quantize("z%d" % c, z[c][:].rearrange("p w t -> p (w t)"), width)
-            per_bank = BANK // width
+            zq = quantize("z%d" % c, z[c][:], width)
+            per_bank = 2 if c == len(CHUNKS) - 1 else BANK // width
             for m0 in range(0, N // P, per_bank):
                 acc = psum.tile([P, BANK], F32, name="acc", tag="acc")
                 for i in range(per_bank):
                     mt = m0 + i
                     product(w3q, slice(mt * P, (mt + 1) * P), zq, slice(0, width), acc[:, i * width : (i + 1) * width])
-                res = sb("res_%d_%d" % (c, m0), [P, BANK], F32)
-                copy = nc.vector.tensor_copy if c >= len(CHUNKS) - 2 else nc.scalar.copy
-                copy(res[:], acc[:])
+                res = sb("res_%d_%d" % (c, m0), [P, per_bank * width], F32)
+                copy = nc.vector.tensor_copy if c == len(CHUNKS) - 1 and m0 > 0 else nc.scalar.copy
+                copy(res[:], acc[:, 0 : per_bank * width])
                 nc.sync.dma_start(
                     out_rows[:, m0 : m0 + per_bank, cols], res[:].rearrange("p (i w) -> p i w", w=width)
                 )

@@ -18,7 +18,8 @@ P = 128
 PACK = 4
 HALF = S // 2
 BANK = 512
-CHUNKS = (256, 256, 256, 128, 128)
+GROUP = 256
+PART = 128
 
 
 def tile_picked_tsketch_none_p_kernel(
@@ -47,8 +48,8 @@ def tile_picked_tsketch_none_p_kernel(
         s2 = [None] + [sb("s2_%d" % t, [P, U], F32) for t in range(1, PACK)]
 
         nc.vector.memset(xs_all[:].bitcast(I32), 0)
-        nc.sync.dma_start(offs_sb[:], offs)
         nc.sync.dma_start(w1_raw[:], w1.rearrange("(p j) c -> p j c", j=PACK))
+        nc.sync.dma_start(offs_sb[:], offs)
         for q in range(4):
             nc.sync.dma_start(
                 xs_all[32 * q : 32 * q + 4, :].bitcast(I32), x_scales[0, 4 * q : 4 * q + 4, :].bitcast(I32)
@@ -110,7 +111,9 @@ def tile_picked_tsketch_none_p_kernel(
 
         def project(name, weights, t, lo, hi, vals=None):
             acc = psum.tile([P, BANK], F32, name="acc", tag="acc")
-            product(weights, slice(t * P, (t + 1) * P), xq, slice(lo, hi), acc[:, 0 : hi - lo])
+            cuts = [lo, HALF, hi] if 0 < lo < HALF < hi else [lo, hi]
+            for a, z in zip(cuts, cuts[1:]):
+                product(weights, slice(t * P, (t + 1) * P), xq, slice(a, z), acc[:, a - lo : z - lo])
             if vals is None:
                 tile = sb(name, [P, hi - lo], F32)
                 vals = tile[:]
@@ -120,10 +123,8 @@ def tile_picked_tsketch_none_p_kernel(
         def scatter(window, lists, vals, lo, hi):
             nc.vector.tensor_copy(window[:].indirect(lists[:, lo // 16 : hi // 16]), vals)
 
-        for h in range(2):
-            for t in (2, 3):
-                lo, hi = h * HALF, (h + 1) * HALF
-                scatter(s1[t], h1_sb, project("y%d_%d" % (t, h), w1q, t, lo, hi), lo, hi)
+        for t, lo, hi in ((2, 0, P), (3, 0, HALF), (2, P, S), (3, HALF, S)):
+            scatter(s1[t], h1_sb, project("y%d_%d" % (t, lo), w1q, t, lo, hi), lo, hi)
 
         w2_bf = sb("w2_bf", [P, PACK * H], BF16)
         deal(nc.scalar.copy, w2_bf, w2_raw, 0, 2)
@@ -150,37 +151,31 @@ def tile_picked_tsketch_none_p_kernel(
             nc.scalar.copy(s1[0][:, t * U : (t + 1) * U], s2[t][:])
         scatter(s1[0], h1_sb, y0, 0, S)
 
-        starts = [sum(CHUNKS[:c]) for c in range(len(CHUNKS))]
-        z = [sb("z_%d" % c, [P, width * PACK], BF16) for c, width in enumerate(CHUNKS)]
+        z = [sb("z_%d" % c, [P, PART * PACK], BF16) for c in range(U // PART)]
         left = s1[0][:].rearrange("p (t a i) -> p a t i", t=PACK, i=4)
         right = s2[0][:].rearrange("p (t a i) -> p a t i", t=PACK, i=4)
         out_rows = out.rearrange("(mt p) w -> p mt w", p=P)
-
-        def multiply(c):
-            quads = slice(starts[c] // 4, (starts[c] + CHUNKS[c]) // 4)
-            nc.vector.tensor_tensor(
-                z[c][:].rearrange("p (a i t) -> p a t i", t=PACK, i=4), left[:, quads], right[:, quads], MULT
-            )
-
-        def layer(c):
-            width = CHUNKS[c]
-            cols = slice(starts[c], starts[c] + width)
-            zq = quantize("z%d" % c, z[c][:], width)
-            per_bank = 2 if c == len(CHUNKS) - 1 else BANK // width
+        groups = U // GROUP
+        for g in range(groups):
+            parts = (2 * g, 2 * g + 1)
+            for c in parts:
+                quads = slice(c * PART // 4, (c + 1) * PART // 4)
+                nc.vector.tensor_tensor(
+                    z[c][:].rearrange("p (a i t) -> p a t i", t=PACK, i=4), left[:, quads], right[:, quads], MULT
+                )
+            zq = planes("z%d" % g, GROUP)
+            for i, c in enumerate(parts):
+                quantize_into(zq, i * PART, (i + 1) * PART, z[c][:])
+            per_bank = 1 if g in (0, groups - 1) else 2
             for m0 in range(0, N // P, per_bank):
                 acc = psum.tile([P, BANK], F32, name="acc", tag="acc")
                 for i in range(per_bank):
                     mt = m0 + i
-                    product(w3q, slice(mt * P, (mt + 1) * P), zq, slice(0, width), acc[:, i * width : (i + 1) * width])
-                res = sb("res_%d_%d" % (c, m0), [P, per_bank * width], F32)
-                copy = nc.vector.tensor_copy if c == len(CHUNKS) - 1 and m0 > 0 else nc.scalar.copy
-                copy(res[:], acc[:, 0 : per_bank * width])
+                    product(w3q, slice(mt * P, (mt + 1) * P), zq, slice(0, GROUP), acc[:, i * GROUP : (i + 1) * GROUP])
+                res = sb("res_%d_%d" % (g, m0), [P, per_bank * GROUP], F32)
+                copy = nc.vector.tensor_copy if g == groups - 1 and m0 % 2 == 0 else nc.scalar.copy
+                copy(res[:], acc[:, 0 : per_bank * GROUP])
                 nc.sync.dma_start(
-                    out_rows[:, m0 : m0 + per_bank, cols], res[:].rearrange("p (i w) -> p i w", w=width)
+                    out_rows[:, m0 : m0 + per_bank, g * GROUP : (g + 1) * GROUP],
+                    res[:].rearrange("p (i w) -> p i w", w=GROUP),
                 )
-
-        multiply(0)
-        for c in range(1, len(CHUNKS)):
-            multiply(c)
-            layer(c - 1)
-        layer(len(CHUNKS) - 1)

@@ -63,8 +63,10 @@ def tile_picked_tsketch_none_p_kernel(
             nc.sync.dma_start(w3_raw[:, t, :], plane_rows(w3, t))
         for t in (2, 1):
             nc.sync.dma_start(s2[t][:], plane_rows(one, t))
-        for t in (2, 3, 1, 0):
+        for t in (2, 3):
             nc.vector.memset(s1[t][:, 0:U], 0.0)
+        for t in (1, 0):
+            nc.gpsimd.memset(s1[t][:, 0:U], 0.0)
 
         def planes(name, width):
             return sb(name + "_codes", [P, width], U32), sb(name + "_scales", [P, width], U8)
@@ -83,37 +85,39 @@ def tile_picked_tsketch_none_p_kernel(
                 raw[:].rearrange("p j (g t r) -> p t g r j", t=PACK, r=8)[:, t0:t1],
             )
 
-        def product(weights, cols, moving, mcols, acc):
+        def product(weights, cols, codes, scales, acc):
             nc.tensor.matmul_mx(
                 out=acc,
                 lhsT=weights[0][:, cols].bitcast(FP8X4),
                 lhsT_scale=weights[1][:, cols],
-                rhs=moving[0][:, mcols].bitcast(FP8X4),
-                rhs_scale=moving[1][:, mcols],
+                rhs=codes.bitcast(FP8X4),
+                rhs_scale=scales,
                 start=True,
                 stop=True,
             )
 
         xs = sb("xs", [P, S], U8)
-        xw = sb("xw", [P, S], U32)
+        xw = [sb("xw_%d" % h, [P, HALF], U32) for h in range(2)]
         nc.vector.tensor_copy(xs[:], xs_all[:].indirect(offs_sb[:]))
         w1_bf = sb("w1_bf", [P, PACK * H], BF16)
         w1q = planes("w1", H)
-        deal(nc.vector.tensor_copy, w1_bf, w1_raw, 2, 4)
+        deal(nc.vector.tensor_copy, w1_bf, w1_raw, 2, 3)
+        deal(nc.scalar.copy, w1_bf, w1_raw, 3, 4)
         quantize_into(w1q, H // 2, H, w1_bf[:, 2 * H : 4 * H])
         deal(nc.scalar.copy, w1_bf, w1_raw, 0, 2)
-        quantize_into(w1q, 0, H // 2, w1_bf[:, 0 : 2 * H])
         for h in range(2):
             nc.vector.tensor_copy(
-                xw[:, h * HALF : (h + 1) * HALF], xw_all[:].indirect(offs_sb[:, h * 16 : (h + 1) * 16])
+                xw[h][:], xw_all[:].indirect(offs_sb[:, h * 16 : (h + 1) * 16])
             )
-        xq = (xw, xs)
+        quantize_into(w1q, 0, H // 2, w1_bf[:, 0 : 2 * H])
 
         def project(name, weights, t, lo, hi, vals=None):
             acc = psum.tile([P, BANK], F32, name="acc", tag="acc")
-            cuts = [lo, HALF, hi] if 0 < lo < HALF < hi else [lo, hi]
+            cuts = [lo, HALF, hi] if lo < HALF < hi else [lo, hi]
             for a, z in zip(cuts, cuts[1:]):
-                product(weights, slice(t * P, (t + 1) * P), xq, slice(a, z), acc[:, a - lo : z - lo])
+                h = a // HALF
+                codes = xw[h][:, a - h * HALF : z - h * HALF]
+                product(weights, slice(t * P, (t + 1) * P), codes, xs[:, a:z], acc[:, a - lo : z - lo])
             if vals is None:
                 tile = sb(name, [P, hi - lo], F32)
                 vals = tile[:]
@@ -151,13 +155,13 @@ def tile_picked_tsketch_none_p_kernel(
             nc.scalar.copy(s1[0][:, t * U : (t + 1) * U], s2[t][:])
         scatter(s1[0], h1_sb, y0, 0, S)
 
-        z = [sb("z_%d" % c, [P, PART * PACK], BF16) for c in range(U // PART)]
         left = s1[0][:].rearrange("p (t a i) -> p a t i", t=PACK, i=4)
         right = s2[0][:].rearrange("p (t a i) -> p a t i", t=PACK, i=4)
         out_rows = out.rearrange("(mt p) w -> p mt w", p=P)
         groups = U // GROUP
         for g in range(groups):
             parts = (2 * g, 2 * g + 1)
+            z = {c: sb("z_%d" % c, [P, PART * PACK], BF16) for c in parts}
             for c in parts:
                 quads = slice(c * PART // 4, (c + 1) * PART // 4)
                 nc.vector.tensor_tensor(
@@ -171,7 +175,7 @@ def tile_picked_tsketch_none_p_kernel(
                 acc = psum.tile([P, BANK], F32, name="acc", tag="acc")
                 for i in range(per_bank):
                     mt = m0 + i
-                    product(w3q, slice(mt * P, (mt + 1) * P), zq, slice(0, GROUP), acc[:, i * GROUP : (i + 1) * GROUP])
+                    product(w3q, slice(mt * P, (mt + 1) * P), zq[0][:], zq[1][:], acc[:, i * GROUP : (i + 1) * GROUP])
                 res = sb("res_%d_%d" % (g, m0), [P, per_bank * GROUP], F32)
                 copy = nc.vector.tensor_copy if g == groups - 1 and m0 % 2 == 0 else nc.scalar.copy
                 copy(res[:], acc[:, 0 : per_bank * GROUP])

@@ -63,10 +63,8 @@ def tile_picked_tsketch_none_p_kernel(
             nc.sync.dma_start(w3_raw[:, t, :], plane_rows(w3, t))
         for t in (2, 1):
             nc.sync.dma_start(s2[t][:], plane_rows(one, t))
-        for t in (2, 3):
+        for t in (2, 3, 1, 0):
             nc.vector.memset(s1[t][:, 0:U], 0.0)
-        for t in (1, 0):
-            nc.gpsimd.memset(s1[t][:, 0:U], 0.0)
 
         def planes(name, width):
             return sb(name + "_codes", [P, width], U32), sb(name + "_scales", [P, width], U8)
@@ -98,13 +96,13 @@ def tile_picked_tsketch_none_p_kernel(
 
         xs = sb("xs", [P, S], U8)
         xw = [sb("xw_%d" % h, [P, HALF], U32) for h in range(2)]
-        nc.vector.tensor_copy(xs[:], xs_all[:].indirect(offs_sb[:]))
         w1_bf = sb("w1_bf", [P, PACK * H], BF16)
         w1q = planes("w1", H)
         deal(nc.vector.tensor_copy, w1_bf, w1_raw, 2, 3)
         deal(nc.scalar.copy, w1_bf, w1_raw, 3, 4)
         quantize_into(w1q, H // 2, H, w1_bf[:, 2 * H : 4 * H])
         deal(nc.scalar.copy, w1_bf, w1_raw, 0, 2)
+        nc.vector.tensor_copy(xs[:], xs_all[:].indirect(offs_sb[:]))
         for h in range(2):
             nc.vector.tensor_copy(
                 xw[h][:], xw_all[:].indirect(offs_sb[:, h * 16 : (h + 1) * 16])
@@ -170,16 +168,16 @@ def tile_picked_tsketch_none_p_kernel(
             zq = planes("z%d" % g, GROUP)
             for i, c in enumerate(parts):
                 quantize_into(zq, i * PART, (i + 1) * PART, z[c][:])
-            per_bank = 1 if g in (0, groups - 1) else 2
-            for m0 in range(0, N // P, per_bank):
-                acc = psum.tile([P, BANK], F32, name="acc", tag="acc")
-                for i in range(per_bank):
+            per_store = 1 if g in (0, groups - 1) else 2
+            for m0 in range(0, N // P, per_store):
+                res = sb("res_%d_%d" % (g, m0), [P, per_store * GROUP], F32)
+                for i in range(per_store):
                     mt = m0 + i
-                    product(w3q, slice(mt * P, (mt + 1) * P), zq[0][:], zq[1][:], acc[:, i * GROUP : (i + 1) * GROUP])
-                res = sb("res_%d_%d" % (g, m0), [P, per_bank * GROUP], F32)
-                copy = nc.vector.tensor_copy if g == groups - 1 and m0 % 2 == 0 else nc.scalar.copy
-                copy(res[:], acc[:, 0 : per_bank * GROUP])
+                    acc = psum.tile([P, BANK], F32, name="acc", tag="acc")
+                    product(w3q, slice(mt * P, (mt + 1) * P), zq[0][:], zq[1][:], acc[:, 0:GROUP])
+                    copy = nc.vector.tensor_copy if g == groups - 1 and mt % 2 == 0 else nc.scalar.copy
+                    copy(res[:, i * GROUP : (i + 1) * GROUP], acc[:, 0:GROUP])
                 nc.sync.dma_start(
-                    out_rows[:, m0 : m0 + per_bank, g * GROUP : (g + 1) * GROUP],
+                    out_rows[:, m0 : m0 + per_store, g * GROUP : (g + 1) * GROUP],
                     res[:].rearrange("p (i w) -> p i w", w=GROUP),
                 )

from contextlib import ExitStack

import concourse.mybir as mybir

K, T, S, N, U, H = 512, 2048, 512, 512, 1024, 512
FLOPS = 2 * (2 * K * H * S + H * N * U)

F32 = mybir.dt.float32
BF16 = mybir.dt.bfloat16
I32 = mybir.dt.int32
U32 = mybir.dt.uint32
U16 = mybir.dt.uint16
U8 = mybir.dt.uint8
FP8X4 = mybir.dt.float8_e4m3fn_x4
MULT = mybir.AluOpType.mult

P = 128
PACK = 4
HALF = S // 2
BANK = 512
GROUP = 256
PART = 128


def tile_picked_tsketch_none_p_kernel(
    tc, x_words, x_scales, w1, w2, one, w3, offs, h1, h2, out
):
    nc = tc.nc
    with ExitStack() as ctx:
        keep = ctx.enter_context(tc.tile_pool(name="keep", bufs=1))
        psum = ctx.enter_context(tc.psum_pool(name="psum", bufs=8))

        def sb(name, shape, dtype, tag=None):
            return keep.tile(shape, dtype, name=name, tag=tag or name, align_bytes=64)

        def plane_rows(a, t):
            return a.rearrange("(g t r) c -> t g r c", t=PACK, r=8)[t]

        offs_sb = keep.tile([P, S // 16], U16, name="offs_sb")
        h1_sb = keep.tile([P, S // 16], U16, name="h1_sb")
        h2_sb = keep.tile([P, S // 16], U16, name="h2_sb")
        xs_all = sb("xs_all", [P, T], U8)
        xw_all = sb("xw_all", [P, T], U32)
        w1_raw = sb("w1_raw", [P, PACK, H], F32)
        w2_raw = sb("w2_raw", [P, PACK, H], F32, tag="w2_then_s2")
        w3_raw = sb("w3_raw", [P, PACK, N], F32)
        s1 = [sb("s1_%d" % t, [P, PACK * U if t == 0 else U], F32) for t in range(PACK)]
        s2 = [None] + [sb("s2_%d" % t, [P, U], F32) for t in range(1, PACK)]

        nc.vector.memset(xs_all[:].bitcast(I32), 0)
        nc.sync.dma_start(w1_raw[:], w1.rearrange("(p j) c -> p j c", j=PACK))
        nc.sync.dma_start(offs_sb[:], offs)
        for q in range(4):
            nc.sync.dma_start(
                xs_all[32 * q : 32 * q + 4, :].bitcast(I32), x_scales[0, 4 * q : 4 * q + 4, :].bitcast(I32)
            )
        nc.sync.dma_start(xw_all[:].bitcast(I32), x_words[0].rearrange("p n t -> p (n t)").bitcast(I32))
        nc.sync.dma_start(h1_sb[:], h1)
        nc.sync.dma_start(w2_raw[:], w2.rearrange("(p j) c -> p j c", j=PACK))
        nc.sync.dma_start(h2_sb[:], h2)
        nc.sync.dma_start(s2[3][:], plane_rows(one, 3))
        for t in range(PACK):
            nc.sync.dma_start(w3_raw[:, t, :], plane_rows(w3, t))
        for t in (2, 1):
            nc.sync.dma_start(s2[t][:], plane_rows(one, t))
        for t in (2, 3, 1, 0):
            nc.vector.memset(s1[t][:, 0:U], 0.0)

        def planes(name, width):
            return sb(name + "_codes", [P, width], U32), sb(name + "_scales", [P, width], U8)

        def quantize_into(q, lo, hi, grouped):
            nc.vector.quantize_mx(out=q[0][:, lo:hi].bitcast(FP8X4), scales=q[1][:, lo:hi], in_=grouped)

        def quantize(name, grouped, width):
            q = planes(name, width)
            quantize_into(q, 0, width, grouped)
            return q

        def deal(copy, grouped, raw, t0, t1):
            copy(
                grouped[:].rearrange("p (t g r j) -> p t g r j", t=PACK, r=8, j=PACK)[:, t0:t1],
                raw[:].rearrange("p j (g t r) -> p t g r j", t=PACK, r=8)[:, t0:t1],
            )

        def product(weights, cols, codes, scales, acc):
            nc.tensor.matmul_mx(
                out=acc,
                lhsT=weights[0][:, cols].bitcast(FP8X4),
                lhsT_scale=weights[1][:, cols],
                rhs=codes.bitcast(FP8X4),
                rhs_scale=scales,
                start=True,
                stop=True,
            )

        xs = sb("xs", [P, S], U8)
        xw = [sb("xw_%d" % h, [P, HALF], U32) for h in range(2)]
        w1_bf = sb("w1_bf", [P, PACK * H], BF16)
        w1q = planes("w1", H)
        deal(nc.vector.tensor_copy, w1_bf, w1_raw, 2, 3)
        deal(nc.scalar.copy, w1_bf, w1_raw, 3, 4)
        quantize_into(w1q, H // 2, H, w1_bf[:, 2 * H : 4 * H])
        deal(nc.scalar.copy, w1_bf, w1_raw, 0, 2)
        nc.vector.tensor_copy(xs[:], xs_all[:].indirect(offs_sb[:]))
        for h in range(2):
            nc.vector.tensor_copy(
                xw[h][:], xw_all[:].indirect(offs_sb[:, h * 16 : (h + 1) * 16])
            )
        quantize_into(w1q, 0, H // 2, w1_bf[:, 0 : 2 * H])

        def project(name, weights, t, lo, hi, vals=None):
            acc = psum.tile([P, BANK], F32, name="acc", tag="acc")
            cuts = [lo, HALF, hi] if lo < HALF < hi else [lo, hi]
            for a, z in zip(cuts, cuts[1:]):
                h = a // HALF
                codes = xw[h][:, a - h * HALF : z - h * HALF]
                product(weights, slice(t * P, (t + 1) * P), codes, xs[:, a:z], acc[:, a - lo : z - lo])
            if vals is None:
                tile = sb(name, [P, hi - lo], F32)
                vals = tile[:]
            nc.scalar.copy(vals, acc[:, 0 : hi - lo])
            return vals

        def scatter(window, lists, vals, lo, hi):
            nc.vector.tensor_copy(window[:].indirect(lists[:, lo // 16 : hi // 16]), vals)

        for t, lo, hi in ((2, 0, P), (3, 0, HALF), (2, P, S), (3, HALF, S)):
            scatter(s1[t], h1_sb, project("y%d_%d" % (t, lo), w1q, t, lo, hi), lo, hi)

        w2_bf = sb("w2_bf", [P, PACK * H], BF16)
        deal(nc.scalar.copy, w2_bf, w2_raw, 0, 2)
        deal(nc.scalar.copy, w2_bf, w2_raw, 2, 4)
        w2q = quantize("w2", w2_bf[:], H)
        s2[0] = sb("s2_0", [P, PACK * U], F32, tag="w2_then_s2")
        nc.sync.dma_start(s2[0][:, 0:U], plane_rows(one, 0))
        scatter(s1[1], h1_sb, project("y1", w1q, 1, 0, S, vals=s2[0][:, U : U + S]), 0, S)

        w3_bf = sb("w3_bf", [P, PACK * N], BF16)
        nc.scalar.copy(
            w3_bf[:].rearrange("p (m t) -> p m t", t=PACK), w3_raw[:].rearrange("p t m -> p m t")
        )
        w3q = quantize("w3", w3_bf[:], N)

        for t in (3, 2, 1):
            scatter(s2[t], h2_sb, project("e%d" % t, w2q, t, 0, S), 0, S)
        e0 = project("e0", w2q, 0, 0, S)
        y0 = project("y0", w1q, 0, 0, S)
        for t in (2, 3, 1):
            nc.scalar.copy(s2[0][:, t * U : (t + 1) * U], s1[t][:])
        scatter(s2[0], h2_sb, e0, 0, S)
        for t in (3, 2, 1):
            nc.scalar.copy(s1[0][:, t * U : (t + 1) * U], s2[t][:])
        scatter(s1[0], h1_sb, y0, 0, S)

        left = s1[0][:].rearrange("p (t a i) -> p a t i", t=PACK, i=4)
        right = s2[0][:].rearrange("p (t a i) -> p a t i", t=PACK, i=4)
        out_rows = out.rearrange("(mt p) w -> p mt w", p=P)
        groups = U // GROUP
        for g in range(groups):
            parts = (2 * g, 2 * g + 1)
            z = {c: sb("z_%d" % c, [P, PART * PACK], BF16) for c in parts}
            for c in parts:
                quads = slice(c * PART // 4, (c + 1) * PART // 4)
                nc.vector.tensor_tensor(
                    z[c][:].rearrange("p (a i t) -> p a t i", t=PACK, i=4), left[:, quads], right[:, quads], MULT
                )
            zq = planes("z%d" % g, GROUP)
            for i, c in enumerate(parts):
                quantize_into(zq, i * PART, (i + 1) * PART, z[c][:])
            per_store = 1 if g in (0, groups - 1) else 2
            for m0 in range(0, N // P, per_store):
                res = sb("res_%d_%d" % (g, m0), [P, per_store * GROUP], F32)
                for i in range(per_store):
                    mt = m0 + i
                    acc = psum.tile([P, BANK], F32, name="acc", tag="acc")
                    product(w3q, slice(mt * P, (mt + 1) * P), zq[0][:], zq[1][:], acc[:, 0:GROUP])
                    copy = nc.vector.tensor_copy if g == groups - 1 and mt % 2 == 0 else nc.scalar.copy
                    copy(res[:, i * GROUP : (i + 1) * GROUP], acc[:, 0:GROUP])
                nc.sync.dma_start(
                    out_rows[:, m0 : m0 + per_store, g * GROUP : (g + 1) * GROUP],
                    res[:].rearrange("p (i w) -> p i w", w=GROUP),
                )
